import numpy as np
import ml_dtypes

BF16 = ml_dtypes.bfloat16


def bf(x):
    return np.asarray(x, np.float32).astype(BF16)


def f32(x):
    return np.asarray(x, np.float32)


def f64(x):
    return np.asarray(x).astype(np.float64)


def striped(idx):
    return np.tile(idx.reshape(-1, 16).T, (8, 1))


S, K, M, N, V, D = 2048, 256, 128, 1024, 256, 4


def setup_inputs():
    return {"table": bf(np.random.standard_normal((K, S))), "w": bf(np.random.standard_normal((K, M)) / np.sqrt(K)), "c": f32(1.5 * np.random.standard_normal((1, N))), "b": f32(0.5 * np.random.standard_normal((M, 1))), "offs": striped(np.random.permutation(np.tile(np.arange(S), 2))[:N])}


def reference(table, w, c, b, offs):
    idx = offs[:16].T.reshape(-1)
    y = (f64(w).T @ f64(table)[:, idx]).reshape(M, V, D)
    a = np.exp(f64(c).reshape(V, D))
    a = a / a.sum(axis=1, keepdims=True)
    z = (y * a).sum(axis=2)
    return np.tanh(z + f64(b))

@@ -1,0 +1,83 @@
+import concourse.mybir as mybir
+from concourse.masks import make_identity
+
+F32, BF16, U16 = mybir.dt.float32, mybir.dt.bfloat16, mybir.dt.uint16
+ALU, ACT, AXIS = mybir.AluOpType, mybir.ActivationFunctionType, mybir.AxisListType
+
+P = 128
+DEGREE = 4
+PIECE = 256
+PER_COLUMN = 16
+
+FLOPS = 2 * 256 * 128 * 1024
+
+
+def tile_rows_wbag_tanh_rep_kernel(tc, table, w, c, b, offs, out):
+    nc = tc.nc
+    features, stored = table.shape
+    entries = c.shape[1]
+    blocks = features // P
+    nodes = entries // DEGREE
+    halves = nodes // P
+    pieces = entries // PIECE
+    piece_nodes = PIECE // DEGREE
+
+    with (
+        tc.tile_pool(name="held", bufs=1) as held,
+        tc.psum_pool(name="psum", bufs=1) as psum,
+    ):
+        table_sb = held.tile([P, blocks, stored], BF16, name="table_sb")
+        nc.scalar.dma_start(table_sb[:], table.rearrange("(a p) s -> p a s", p=P))
+        logits = held.tile([P, halves, DEGREE], F32, name="logits")
+        nc.sync.dma_start(logits[:], c.rearrange("o (h p t) -> p (o h) t", p=P, t=DEGREE))
+        offsets = held.tile([P, entries // PER_COLUMN], U16, name="offsets")
+        nc.sync.dma_start(offsets[:], offs)
+        w_sb = held.tile([P, blocks, P], BF16, name="w_sb")
+        nc.sync.dma_start(w_sb[:], w.rearrange("(a p) m -> p a m", p=P))
+        bias = held.tile([P, 1], F32, name="bias")
+        nc.sync.dma_start(bias[:], b)
+        identity = held.tile([P, P], F32, name="identity")
+        make_identity(nc, identity[:])
+
+        wide = [P, halves, DEGREE]
+        largest = held.tile([P, halves], F32, name="largest")
+        nc.vector.tensor_reduce(largest[:], logits[:], AXIS.X, ALU.max)
+        shifted = held.tile(wide, F32, name="shifted")
+        nc.vector.tensor_tensor(shifted[:], logits[:], largest[:].unsqueeze(2).to_broadcast(wide), ALU.subtract)
+        exps = held.tile(wide, F32, name="exps")
+        nc.scalar.activation(exps[:], shifted[:], ACT.Exp)
+        total = held.tile([P, halves], F32, name="total")
+        nc.vector.tensor_reduce(total[:], exps[:], AXIS.X, ALU.add)
+        inverse = held.tile([P, halves], F32, name="inverse")
+        nc.vector.reciprocal(inverse[:], total[:])
+        probs = held.tile(wide, F32, name="probs")
+        nc.vector.tensor_tensor(probs[:], exps[:], inverse[:].unsqueeze(2).to_broadcast(wide), ALU.mult)
+
+        spread = []
+        for h in range(halves):
+            flipped = psum.tile([P, DEGREE, P], F32, name=f"flipped{h}")
+            for t in range(DEGREE):
+                nc.tensor.transpose(flipped[:, t, :], probs[:, h, t:t + 1].to_broadcast([P, P]), identity[:])
+            rows = held.tile([P, P, DEGREE], F32, name=f"rows{h}")
+            in_list_order = flipped[:].rearrange("p t v -> p v t")
+            if h % 2 == 0:
+                nc.vector.tensor_copy(rows[:], in_list_order)
+            else:
+                nc.scalar.copy(rows[:], in_list_order)
+            spread.append(rows)
+
+        for q in range(pieces):
+            picked = offsets[:, q * PIECE // PER_COLUMN:(q + 1) * PIECE // PER_COLUMN]
+            y = psum.tile([P, PIECE], F32, name=f"y{q}")
+            for a in range(blocks):
+                nc.tensor.matmul(y[:], w_sb[:, a, :], table_sb[:, a, :].indirect(picked),
+                                 start=(a == 0), stop=(a == blocks - 1))
+            h, first = divmod(q * piece_nodes, P)
+            weighted = held.tile([P, piece_nodes, DEGREE], F32, name=f"weighted{q}")
+            nc.vector.tensor_tensor(weighted[:], y[:].rearrange("p (v t) -> p v t", t=DEGREE),
+                                    spread[h][:, first:first + piece_nodes, :], ALU.mult)
+            z = held.tile([P, piece_nodes], F32, name=f"z{q}")
+            nc.vector.tensor_reduce(z[:], weighted[:], AXIS.X, ALU.add)
+            result = held.tile([P, piece_nodes], F32, name=f"result{q}")
+            nc.scalar.activation(result[:], z[:], ACT.Tanh, bias=bias[:])
+            nc.sync.dma_start(out[:, q * piece_nodes:(q + 1) * piece_nodes], result[:])

@@ -17,19 +17,20 @@ def tile_rows_wbag_tanh_rep_kernel(tc, table, w, c, b, offs, out):
     features, stored = table.shape
     entries = c.shape[1]
     blocks = features // P
-    nodes = entries // DEGREE
-    halves = nodes // P
+    halves = entries // DEGREE // P
     pieces = entries // PIECE
     piece_nodes = PIECE // DEGREE
+    assert pieces == 2 * halves
 
     with (
         tc.tile_pool(name="held", bufs=1) as held,
-        tc.psum_pool(name="psum", bufs=1) as psum,
+        tc.psum_pool(name="psum", bufs=pieces) as psum,
     ):
         table_sb = held.tile([P, blocks, stored], BF16, name="table_sb")
         nc.scalar.dma_start(table_sb[:], table.rearrange("(a p) s -> p a s", p=P))
-        logits = held.tile([P, halves, DEGREE], F32, name="logits")
-        nc.sync.dma_start(logits[:], c.rearrange("o (h p t) -> p (o h) t", p=P, t=DEGREE))
+        padded = held.tile([P, halves, 2 * DEGREE], F32, name="padded")
+        logits = padded[:, :, :DEGREE]
+        nc.sync.dma_start(logits, c.rearrange("o (h p t) -> p (o h) t", p=P, t=DEGREE))
         offsets = held.tile([P, entries // PER_COLUMN], U16, name="offsets")
         nc.sync.dma_start(offsets[:], offs)
         w_sb = held.tile([P, blocks, P], BF16, name="w_sb")
@@ -39,45 +40,45 @@ def tile_rows_wbag_tanh_rep_kernel(tc, table, w, c, b, offs, out):
         identity = held.tile([P, P], F32, name="identity")
         make_identity(nc, identity[:])
 
-        wide = [P, halves, DEGREE]
-        largest = held.tile([P, halves], F32, name="largest")
-        nc.vector.tensor_reduce(largest[:], logits[:], AXIS.X, ALU.max)
-        shifted = held.tile(wide, F32, name="shifted")
-        nc.vector.tensor_tensor(shifted[:], logits[:], largest[:].unsqueeze(2).to_broadcast(wide), ALU.subtract)
-        exps = held.tile(wide, F32, name="exps")
-        nc.scalar.activation(exps[:], shifted[:], ACT.Exp)
-        total = held.tile([P, halves], F32, name="total")
-        nc.vector.tensor_reduce(total[:], exps[:], AXIS.X, ALU.add)
-        inverse = held.tile([P, halves], F32, name="inverse")
-        nc.vector.reciprocal(inverse[:], total[:])
-        probs = held.tile(wide, F32, name="probs")
-        nc.vector.tensor_tensor(probs[:], exps[:], inverse[:].unsqueeze(2).to_broadcast(wide), ALU.mult)
+        pairs = [P, halves, DEGREE, DEGREE]
+        gaps = held.tile(pairs, F32, name="gaps")
+        nc.vector.tensor_tensor(gaps[:], logits.unsqueeze(2).to_broadcast(pairs),
+                                logits.unsqueeze(3).to_broadcast(pairs), ALU.subtract)
+        ratios = held.tile(pairs, F32, name="ratios")
+        nc.scalar.activation(ratios[:], gaps[:], ACT.Exp)
+        totals = held.tile([P, halves, DEGREE], F32, name="totals")
+        nc.vector.tensor_reduce(totals[:], ratios[:], AXIS.X, ALU.add)
+        probs = held.tile([P, halves, DEGREE], F32, name="probs")
+        nc.vector.reciprocal(probs[:], totals[:])
 
         spread = []
         for h in range(halves):
-            flipped = psum.tile([P, DEGREE, P], F32, name=f"flipped{h}")
-            for t in range(DEGREE):
-                nc.tensor.transpose(flipped[:, t, :], probs[:, h, t:t + 1].to_broadcast([P, P]), identity[:])
-            rows = held.tile([P, P, DEGREE], F32, name=f"rows{h}")
-            in_list_order = flipped[:].rearrange("p t v -> p v t")
-            if h % 2 == 0:
-                nc.vector.tensor_copy(rows[:], in_list_order)
-            else:
-                nc.scalar.copy(rows[:], in_list_order)
+            rows = held.tile([P, 2, P, 2], F32, name=f"rows{h}")
+            for u, copy in enumerate((nc.vector.tensor_copy, nc.scalar.copy)):
+                flipped = psum.tile([P, 2, P], F32, name=f"flipped{h}{u}", tag="bank")
+                for t in range(2):
+                    column = probs[:, h, 2 * u + t:2 * u + t + 1]
+                    nc.tensor.transpose(flipped[:, t, :], column.to_broadcast([P, P]), identity[:])
+                copy(rows[:, u, :, :], flipped[:].rearrange("m t v -> m v t"))
             spread.append(rows)
 
-        for q in range(pieces):
-            picked = offsets[:, q * PIECE // PER_COLUMN:(q + 1) * PIECE // PER_COLUMN]
-            y = psum.tile([P, PIECE], F32, name=f"y{q}")
+        for h in range(halves):
+            both = (2 * h, 2 * h + 1)
+            y = [psum.tile([P, PIECE], F32, name=f"y{q}", tag="bank") for q in both]
             for a in range(blocks):
-                nc.tensor.matmul(y[:], w_sb[:, a, :], table_sb[:, a, :].indirect(picked),
-                                 start=(a == 0), stop=(a == blocks - 1))
-            h, first = divmod(q * piece_nodes, P)
-            weighted = held.tile([P, piece_nodes, DEGREE], F32, name=f"weighted{q}")
-            nc.vector.tensor_tensor(weighted[:], y[:].rearrange("p (v t) -> p v t", t=DEGREE),
-                                    spread[h][:, first:first + piece_nodes, :], ALU.mult)
-            z = held.tile([P, piece_nodes], F32, name=f"z{q}")
-            nc.vector.tensor_reduce(z[:], weighted[:], AXIS.X, ALU.add)
-            result = held.tile([P, piece_nodes], F32, name=f"result{q}")
-            nc.scalar.activation(result[:], z[:], ACT.Tanh, bias=bias[:])
-            nc.sync.dma_start(out[:, q * piece_nodes:(q + 1) * piece_nodes], result[:])
+                for i, q in enumerate(both):
+                    picked = offsets[:, q * PIECE // PER_COLUMN:(q + 1) * PIECE // PER_COLUMN]
+                    nc.tensor.matmul(y[i][:], w_sb[:, a, :], table_sb[:, a, :].indirect(picked),
+                                     start=(a == 0), stop=(a == blocks - 1))
+            weighted = []
+            for i, q in enumerate(both):
+                product = held.tile([P, 2, piece_nodes, 2], F32, name=f"product{q}")
+                nc.vector.tensor_tensor(product[:], y[i][:].rearrange("m (v u t) -> m u v t", u=2, t=2),
+                                        spread[h][:, :, i * piece_nodes:(i + 1) * piece_nodes, :], ALU.mult)
+                weighted.append(product)
+            for i, q in enumerate(both):
+                z = held.tile([P, piece_nodes], F32, name=f"z{q}")
+                nc.vector.tensor_reduce(z[:], weighted[i][:].rearrange("m u v t -> m v u t"), AXIS.XY, ALU.add)
+                result = held.tile([P, piece_nodes], F32, name=f"result{q}")
+                nc.scalar.activation(result[:], z[:], ACT.Tanh, bias=bias[:])
+                nc.sync.dma_start(out[:, q * piece_nodes:(q + 1) * piece_nodes], result[:])

@@ -26,15 +26,16 @@ def tile_rows_wbag_tanh_rep_kernel(tc, table, w, c, b, offs, out):
         tc.tile_pool(name="held", bufs=1) as held,
         tc.psum_pool(name="psum", bufs=pieces) as psum,
     ):
-        table_sb = held.tile([P, blocks, stored], BF16, name="table_sb")
-        nc.scalar.dma_start(table_sb[:], table.rearrange("(a p) s -> p a s", p=P))
         padded = held.tile([P, halves, 2 * DEGREE], F32, name="padded")
         logits = padded[:, :, :DEGREE]
         nc.sync.dma_start(logits, c.rearrange("o (h p t) -> p (o h) t", p=P, t=DEGREE))
+        table_sb = held.tile([P, blocks, stored], BF16, name="table_sb")
+        nc.sync.dma_start(table_sb[:, 0, :], table[:P, :])
         offsets = held.tile([P, entries // PER_COLUMN], U16, name="offsets")
         nc.sync.dma_start(offsets[:], offs)
         w_sb = held.tile([P, blocks, P], BF16, name="w_sb")
         nc.sync.dma_start(w_sb[:], w.rearrange("(a p) m -> p a m", p=P))
+        nc.sync.dma_start(table_sb[:, 1, :], table[P:, :])
         bias = held.tile([P, 1], F32, name="bias")
         nc.sync.dma_start(bias[:], b)
         identity = held.tile([P, P], F32, name="identity")

import concourse.mybir as mybir
from concourse.masks import make_identity

F32, BF16, U16 = mybir.dt.float32, mybir.dt.bfloat16, mybir.dt.uint16
ALU, ACT, AXIS = mybir.AluOpType, mybir.ActivationFunctionType, mybir.AxisListType

P = 128
DEGREE = 4
PIECE = 256
PER_COLUMN = 16

FLOPS = 2 * 256 * 128 * 1024


def tile_rows_wbag_tanh_rep_kernel(tc, table, w, c, b, offs, out):
    nc = tc.nc
    features, stored = table.shape
    entries = c.shape[1]
    blocks = features // P
    halves = entries // DEGREE // P
    pieces = entries // PIECE
    piece_nodes = PIECE // DEGREE
    assert pieces == 2 * halves

    with (
        tc.tile_pool(name="held", bufs=1) as held,
        tc.psum_pool(name="psum", bufs=pieces) as psum,
    ):
        padded = held.tile([P, halves, 2 * DEGREE], F32, name="padded")
        logits = padded[:, :, :DEGREE]
        nc.sync.dma_start(logits, c.rearrange("o (h p t) -> p (o h) t", p=P, t=DEGREE))
        table_sb = held.tile([P, blocks, stored], BF16, name="table_sb")
        nc.sync.dma_start(table_sb[:, 0, :], table[:P, :])
        offsets = held.tile([P, entries // PER_COLUMN], U16, name="offsets")
        nc.sync.dma_start(offsets[:], offs)
        w_sb = held.tile([P, blocks, P], BF16, name="w_sb")
        nc.sync.dma_start(w_sb[:], w.rearrange("(a p) m -> p a m", p=P))
        nc.sync.dma_start(table_sb[:, 1, :], table[P:, :])
        bias = held.tile([P, 1], F32, name="bias")
        nc.sync.dma_start(bias[:], b)
        identity = held.tile([P, P], F32, name="identity")
        make_identity(nc, identity[:])

        pairs = [P, halves, DEGREE, DEGREE]
        gaps = held.tile(pairs, F32, name="gaps")
        nc.vector.tensor_tensor(gaps[:], logits.unsqueeze(2).to_broadcast(pairs),
                                logits.unsqueeze(3).to_broadcast(pairs), ALU.subtract)
        ratios = held.tile(pairs, F32, name="ratios")
        nc.scalar.activation(ratios[:], gaps[:], ACT.Exp)
        totals = held.tile([P, halves, DEGREE], F32, name="totals")
        nc.vector.tensor_reduce(totals[:], ratios[:], AXIS.X, ALU.add)
        probs = held.tile([P, halves, DEGREE], F32, name="probs")
        nc.vector.reciprocal(probs[:], totals[:])

        spread = []
        for h in range(halves):
            rows = held.tile([P, 2, P, 2], F32, name=f"rows{h}")
            for u, copy in enumerate((nc.vector.tensor_copy, nc.scalar.copy)):
                flipped = psum.tile([P, 2, P], F32, name=f"flipped{h}{u}", tag="bank")
                for t in range(2):
                    column = probs[:, h, 2 * u + t:2 * u + t + 1]
                    nc.tensor.transpose(flipped[:, t, :], column.to_broadcast([P, P]), identity[:])
                copy(rows[:, u, :, :], flipped[:].rearrange("m t v -> m v t"))
            spread.append(rows)

        for h in range(halves):
            both = (2 * h, 2 * h + 1)
            y = [psum.tile([P, PIECE], F32, name=f"y{q}", tag="bank") for q in both]
            for a in range(blocks):
                for i, q in enumerate(both):
                    picked = offsets[:, q * PIECE // PER_COLUMN:(q + 1) * PIECE // PER_COLUMN]
                    nc.tensor.matmul(y[i][:], w_sb[:, a, :], table_sb[:, a, :].indirect(picked),
                                     start=(a == 0), stop=(a == blocks - 1))
            weighted = []
            for i, q in enumerate(both):
                product = held.tile([P, 2, piece_nodes, 2], F32, name=f"product{q}")
                nc.vector.tensor_tensor(product[:], y[i][:].rearrange("m (v u t) -> m u v t", u=2, t=2),
                                        spread[h][:, :, i * piece_nodes:(i + 1) * piece_nodes, :], ALU.mult)
                weighted.append(product)
            for i, q in enumerate(both):
                z = held.tile([P, piece_nodes], F32, name=f"z{q}")
                nc.vector.tensor_reduce(z[:], weighted[i][:].rearrange("m u v t -> m v u t"), AXIS.XY, ALU.add)
                result = held.tile([P, piece_nodes], F32, name=f"result{q}")
                nc.scalar.activation(result[:], z[:], ACT.Tanh, bias=bias[:])
                nc.sync.dma_start(out[:, q * piece_nodes:(q + 1) * piece_nodes], result[:])
